import numpy as np
import ml_dtypes


def mxq(x, axis, fmt="e4m3"):
    dtype, down = {"e4m3": (ml_dtypes.float8_e4m3fn, 7), "e5m2": (ml_dtypes.float8_e5m2, 14)}[fmt]
    v = np.moveaxis(np.asarray(x, np.float32).astype(ml_dtypes.bfloat16).astype(np.float64), axis, -1)
    blocks = v.reshape(v.shape[:-1] + (-1, 32))
    amax = np.abs(blocks).max(-1, keepdims=True)
    byte = np.maximum(np.where(amax > 0, np.frexp(amax)[1] - 1 + 127, 0) - down, 1)
    scale = np.exp2(byte - 127.0)
    codes = (blocks / scale).astype(np.float32).astype(dtype).astype(np.float64)
    return np.moveaxis((codes * scale).reshape(v.shape), -1, axis)


WIDE = False


def mx_kscale(k):
    if not WIDE:
        return np.ones(k)
    levels = np.array([10, -10, 5, -5, 0])
    if k % 512:
        return np.exp2(np.random.permutation(np.resize(levels, k // 32))).repeat(32)
    a = np.empty((k // 512, 16))
    for p in range(k // 512):
        a[p, :8] = np.random.permutation(np.resize(levels, 8))
        for g in range(8):
            far = levels[np.abs(levels - a[p, g]) >= 10]
            a[p, g + 8] = far[np.random.randint(len(far))]
    return np.exp2(a.ravel()).repeat(32)


def f64(x):
    return np.asarray(x).astype(np.float64)


def striped(idx):
    return np.tile(idx.reshape(-1, 16).T, (8, 1)).astype(np.uint16)


def unstriped(offs):
    return offs[:16].T.reshape(-1).astype(np.int64)


def pack_weight(w):
    k, n = w.shape
    w = f64(np.asarray(w, np.float32).astype(ml_dtypes.bfloat16)).reshape(k // 32, 32, n)
    amax = np.abs(w).max(1)
    byte = np.clip(np.where(amax > 0, np.frexp(amax)[1] - 1 + 127 - 7, 1), 1, 254)
    scaled = (w * np.exp2(127.0 - byte)[:, None, :]).reshape(k, n).astype(np.float32)
    words = np.ascontiguousarray(scaled.reshape(k // 512, 128, 4, n).transpose(0, 1, 3, 2)).astype(ml_dtypes.float8_e4m3fn).view(np.uint8)
    return words, np.ascontiguousarray(byte.astype(np.uint8).reshape(k // 512, 16, n))


def unpack_weight(words, scales):
    g, p, n, _ = words.shape
    vals = np.ascontiguousarray(words).view(ml_dtypes.float8_e4m3fn).astype(np.float64) * np.repeat(np.exp2(scales.astype(np.float64) - 127.0), 8, axis=1)[..., None]
    return vals.transpose(0, 1, 3, 2).reshape(g * 512, n)


def relu(v):
    return np.maximum(v, 0.0)


K, T, S, N = 512, 4096, 1024, 128
P = 2 ** 7


def setup_inputs():
    n = np.random.standard_normal
    s = mx_kscale(K)[:, None]
    packed_w1 = pack_weight(n((K, N)) / np.sqrt(K) / s)
    return {
        "xT": (n((K, T)) * s).astype(np.float32),
        "tscale": np.tile(np.random.uniform(0.25, 2.0, T), (P, 1)).astype(np.float32),
        "cscale": np.random.uniform(0.5, 1.5, (N, 1)).astype(np.float32),
        "w1_words": packed_w1[0],
        "w1_scales": packed_w1[1],
        "offs": striped(np.random.permutation(T)[:S]),
    }


def reference(xT, tscale, cscale, w1_words, w1_scales, offs):
    xq = mxq(f64(xT)[:, unstriped(offs)], 0, "e4m3")
    y = unpack_weight(w1_words, w1_scales).T @ xq
    tg = f64(tscale)[:1][:, unstriped(offs)]
    return relu((f64(cscale) * y) * tg)

@@ -1,0 +1,110 @@
+from contextlib import ExitStack
+
+import concourse.mybir as mybir
+from concourse.masks import make_identity
+
+K, T, S, N = 512, 4096, 1024, 128
+FLOPS = 2 * K * S * N
+BYTES = 4 * K * T + 4 * T + 4 * N + K * N + 16 * N + 2 * 128 * (S // 16) + 4 * N * S
+
+F32 = mybir.dt.float32
+BF16 = mybir.dt.bfloat16
+I32 = mybir.dt.int32
+U32 = mybir.dt.uint32
+U16 = mybir.dt.uint16
+U8 = mybir.dt.uint8
+FP8X4 = mybir.dt.float8_e4m3fn_x4
+MULT = mybir.AluOpType.mult
+COPY = mybir.ActivationFunctionType.Copy
+RELU = mybir.ActivationFunctionType.Relu
+
+P = 128
+PACK = 4
+HALF = S // 2
+PIECE = 256
+RUN = T // P
+LAST_CHUNKS = ((0, 1024), (1024, 2048), (2048, 3072), (3072, 3584), (3584, 4096))
+VECTOR_CHUNK = 2
+
+
+def tile_picked_tokscale_relu_l_kernel(tc, xT, tscale, cscale, w1_words, w1_scales, offs, out):
+    nc = tc.nc
+    with ExitStack() as ctx:
+        keep = ctx.enter_context(tc.tile_pool(name="keep", bufs=1))
+        spread = ctx.enter_context(tc.psum_pool(name="spread", bufs=4))
+        sums = ctx.enter_context(tc.psum_pool(name="sums", bufs=1))
+
+        offsets = keep.tile([P, S // 16], U16, name="offsets")
+        planes = [keep.tile([P, T], F32, name=f"plane{t}") for t in range(PACK)]
+        x_rows = xT.rearrange("(p t) w -> p t w", t=PACK)
+
+        nc.sync.dma_start(planes[0][:], x_rows[:, 0, :])
+        nc.sync.dma_start(offsets[:], offs)
+        for t in range(1, PACK - 1):
+            nc.sync.dma_start(planes[t][:], x_rows[:, t, :])
+        for a, b in LAST_CHUNKS:
+            nc.sync.dma_start(planes[PACK - 1][:, a:b], x_rows[:, PACK - 1, a:b])
+
+        ts_runs = keep.tile([P, RUN], F32, name="ts_runs")
+        nc.scalar.dma_start(ts_runs[:], tscale[0].rearrange("(p c) -> p c", c=RUN))
+
+        identity = keep.tile([P, P], F32, name="identity")
+        make_identity(nc, identity[:])
+
+        w_codes = keep.tile([P, N], U32, name="w_codes", align_bytes=64)
+        w_scales = keep.tile([P, N], U8, name="w_scales", align_bytes=64)
+        c_col = keep.tile([P, 1], F32, name="c_col")
+        nc.gpsimd.memset(w_scales[:].bitcast(U32), 0)
+        nc.gpsimd.dma_start(w_codes[:].bitcast(I32), w1_words[0].rearrange("p n t -> p (n t)").bitcast(I32))
+        nc.gpsimd.dma_start(c_col[:], cscale)
+        for q in range(4):
+            nc.gpsimd.dma_start(w_scales[32 * q : 32 * q + 4, :].bitcast(I32), w1_scales[0, 4 * q : 4 * q + 4, :].bitcast(I32))
+
+        ts_window = keep.tile([P, T], F32, name="ts_window")
+        ts_view = ts_window[:].rearrange("m (p c) -> m p c", c=RUN)
+        for b in range(RUN // 4):
+            bank = spread.tile([P, 4, P], F32, name="bank")
+            for i in range(4):
+                c = 4 * b + i
+                nc.tensor.transpose(bank[:, i, :], ts_runs[:, c : c + 1].to_broadcast([P, P]), identity[:])
+            nc.scalar.activation(ts_view[:, :, 4 * b : 4 * b + 4], bank[:].rearrange("m i p -> m p i"), COPY)
+
+        halves = [offsets[:, h * (HALF // 16) : (h + 1) * (HALF // 16)] for h in range(2)]
+        grouped = [keep.tile([P, HALF, PACK], BF16, name=f"grouped{h}", align_bytes=64) for h in range(2)]
+        ts_picked = keep.tile([P, S], F32, name="ts_picked")
+
+        for t in range(PACK - 1):
+            for h in range(2):
+                nc.vector.tensor_copy(grouped[h][:, :, t], planes[t][:].indirect(halves[h]))
+            if t == 0:
+                nc.vector.tensor_copy(ts_picked[:], ts_window[:].indirect(offsets[:]))
+
+        last_bf16 = keep.tile([P, T], BF16, name="last_bf16")
+        for i, (a, b) in enumerate(LAST_CHUNKS):
+            if i == VECTOR_CHUNK:
+                nc.vector.tensor_copy(last_bf16[:, a:b], planes[PACK - 1][:, a:b])
+            else:
+                nc.scalar.copy(last_bf16[:, a:b], planes[PACK - 1][:, a:b])
+        nc.vector.tensor_copy(grouped[0][:, :, PACK - 1], planes[PACK - 1][:].indirect(halves[0]))
+        nc.scalar.activation(grouped[1][:, :, PACK - 1], last_bf16[:].indirect(halves[1]), COPY)
+
+        for h in range(2):
+            accs = []
+            for j in range(HALF // PIECE):
+                u = h * (HALF // PIECE) + j
+                codes = keep.tile([P, PIECE], U32, name=f"codes{u}", align_bytes=64)
+                scales = keep.tile([P, PIECE], U8, name=f"scales{u}", align_bytes=64)
+                src = grouped[h][:].rearrange("p n t -> p (n t)")[:, j * PIECE * PACK : (j + 1) * PIECE * PACK]
+                nc.vector.quantize_mx(out=codes[:].bitcast(FP8X4), scales=scales[:], in_=src)
+                acc = sums.tile([P, PIECE], F32, name=f"acc{u}")
+                nc.tensor.matmul_mx(out=acc[:], lhsT=w_codes[:].bitcast(FP8X4), lhsT_scale=w_scales[:],
+                                    rhs=codes[:].bitcast(FP8X4), rhs_scale=scales[:], start=True, stop=True)
+                accs.append(acc)
+            for j, acc in enumerate(accs):
+                u = h * (HALF // PIECE) + j
+                cols = slice(u * PIECE, (u + 1) * PIECE)
+                scaled = keep.tile([P, PIECE], F32, name=f"scaled{u}")
+                nc.vector.scalar_tensor_tensor(scaled[:], acc[:], c_col[:], ts_picked[:, cols], MULT, MULT)
+                result = keep.tile([P, PIECE], F32, name=f"result{u}")
+                nc.scalar.activation(result[:], scaled[:], RELU)
+                nc.sync.dma_start(out[:, cols], result[:])

@@ -21,47 +21,51 @@ RELU = mybir.ActivationFunctionType.Relu
 P = 128
 PACK = 4
 HALF = S // 2
-PIECE = 256
+PIECES = ((256, 256), (256, 128, 128))
 RUN = T // P
-LAST_CHUNKS = ((0, 1024), (1024, 2048), (2048, 3072), (3072, 3584), (3584, 4096))
-VECTOR_CHUNK = 2
+LAST_CHUNKS = ((0, 1024), (1024, 2048), (2048, 3072), (3072, 3584), (3584, 3840), (3840, 4096))
+VECTOR_CHUNKS = (2, 3)
 
 
 def tile_picked_tokscale_relu_l_kernel(tc, xT, tscale, cscale, w1_words, w1_scales, offs, out):
     nc = tc.nc
     with ExitStack() as ctx:
         keep = ctx.enter_context(tc.tile_pool(name="keep", bufs=1))
-        spread = ctx.enter_context(tc.psum_pool(name="spread", bufs=4))
+        spread = ctx.enter_context(tc.psum_pool(name="spread", bufs=3))
         sums = ctx.enter_context(tc.psum_pool(name="sums", bufs=1))
 
         offsets = keep.tile([P, S // 16], U16, name="offsets")
-        planes = [keep.tile([P, T], F32, name=f"plane{t}") for t in range(PACK)]
+        shared = keep.tile([P, 2 * T + HALF], F32, name="shared", align_bytes=64)
+        ts_window = shared[:, 0:T]
+        grouped = shared[:, 0 : S * PACK // 2].bitcast(BF16).rearrange("p (n t) -> p n t", t=PACK)
+        pair = shared[:, T - HALF : T + HALF].rearrange("p (t n) -> p t n", t=2)
+        last_bf16 = shared[:, T - HALF : T - HALF + T // 2].bitcast(BF16)
+        planes = [keep.tile([P, T], F32, name=f"plane{t}")[:] if t != 2 else shared[:, T + HALF :] for t in range(PACK)]
         x_rows = xT.rearrange("(p t) w -> p t w", t=PACK)
 
-        nc.sync.dma_start(planes[0][:], x_rows[:, 0, :])
+        ts_runs = keep.tile([P, RUN], F32, name="ts_runs")
+        w_codes = keep.tile([P, N], U32, name="w_codes", align_bytes=64)
+        w_scales = keep.tile([P, N], U8, name="w_scales", align_bytes=64)
+        c_col = keep.tile([P, 1], F32, name="c_col")
+
+        nc.vector.memset(w_scales[:].bitcast(U32), 0)
+
+        nc.sync.dma_start(ts_runs[:], tscale[0].rearrange("(p c) -> p c", c=RUN))
+        nc.sync.dma_start(planes[1], x_rows[:, 1, :])
         nc.sync.dma_start(offsets[:], offs)
-        for t in range(1, PACK - 1):
-            nc.sync.dma_start(planes[t][:], x_rows[:, t, :])
+        nc.sync.dma_start(planes[0], x_rows[:, 0, :])
+        for q in range(4):
+            nc.sync.dma_start(w_scales[32 * q : 32 * q + 4, :].bitcast(I32), w1_scales[0, 4 * q : 4 * q + 4, :].bitcast(I32))
+        nc.sync.dma_start(planes[2], x_rows[:, 2, :])
         for a, b in LAST_CHUNKS:
             nc.sync.dma_start(planes[PACK - 1][:, a:b], x_rows[:, PACK - 1, a:b])
-
-        ts_runs = keep.tile([P, RUN], F32, name="ts_runs")
-        nc.scalar.dma_start(ts_runs[:], tscale[0].rearrange("(p c) -> p c", c=RUN))
+        nc.sync.dma_start(w_codes[:].bitcast(I32), w1_words[0].rearrange("p n t -> p (n t)").bitcast(I32))
+        nc.sync.dma_start(c_col[:], cscale)
 
         identity = keep.tile([P, P], F32, name="identity")
         make_identity(nc, identity[:])
 
-        w_codes = keep.tile([P, N], U32, name="w_codes", align_bytes=64)
-        w_scales = keep.tile([P, N], U8, name="w_scales", align_bytes=64)
-        c_col = keep.tile([P, 1], F32, name="c_col")
-        nc.gpsimd.memset(w_scales[:].bitcast(U32), 0)
-        nc.gpsimd.dma_start(w_codes[:].bitcast(I32), w1_words[0].rearrange("p n t -> p (n t)").bitcast(I32))
-        nc.gpsimd.dma_start(c_col[:], cscale)
-        for q in range(4):
-            nc.gpsimd.dma_start(w_scales[32 * q : 32 * q + 4, :].bitcast(I32), w1_scales[0, 4 * q : 4 * q + 4, :].bitcast(I32))
-
-        ts_window = keep.tile([P, T], F32, name="ts_window")
-        ts_view = ts_window[:].rearrange("m (p c) -> m p c", c=RUN)
+        ts_view = ts_window.rearrange("m (p c) -> m p c", c=RUN)
         for b in range(RUN // 4):
             bank = spread.tile([P, 4, P], F32, name="bank")
             for i in range(4):
@@ -70,41 +74,44 @@ def tile_picked_tokscale_relu_l_kernel(tc, xT, tscale, cscale, w1_words, w1_scal
             nc.scalar.activation(ts_view[:, :, 4 * b : 4 * b + 4], bank[:].rearrange("m i p -> m p i"), COPY)
 
         halves = [offsets[:, h * (HALF // 16) : (h + 1) * (HALF // 16)] for h in range(2)]
-        grouped = [keep.tile([P, HALF, PACK], BF16, name=f"grouped{h}", align_bytes=64) for h in range(2)]
-        ts_picked = keep.tile([P, S], F32, name="ts_picked")
+        ts_picked = [keep.tile([P, HALF], F32, name=f"ts_picked{h}") for h in range(2)]
 
-        for t in range(PACK - 1):
-            for h in range(2):
-                nc.vector.tensor_copy(grouped[h][:, :, t], planes[t][:].indirect(halves[h]))
-            if t == 0:
-                nc.vector.tensor_copy(ts_picked[:], ts_window[:].indirect(offsets[:]))
+        nc.vector.tensor_copy(pair[:, 1, :], planes[1].indirect(halves[1]))
+        for h in range(2):
+            nc.vector.tensor_copy(ts_picked[h][:], ts_window.indirect(halves[h]))
+        nc.vector.tensor_copy(grouped[:, :HALF, 1], planes[1].indirect(halves[0]))
+        nc.vector.tensor_copy(pair[:, 0, :], planes[0].indirect(halves[1]))
+        nc.vector.tensor_copy(grouped[:, :HALF, 0], planes[0].indirect(halves[0]))
+        nc.scalar.copy(grouped[:, HALF:, 0:2], pair.rearrange("p t n -> p n t"))
+        nc.vector.tensor_copy(grouped[:, :, 2], planes[2].indirect(offsets[:]))
 
-        last_bf16 = keep.tile([P, T], BF16, name="last_bf16")
         for i, (a, b) in enumerate(LAST_CHUNKS):
-            if i == VECTOR_CHUNK:
+            if i in VECTOR_CHUNKS:
                 nc.vector.tensor_copy(last_bf16[:, a:b], planes[PACK - 1][:, a:b])
             else:
                 nc.scalar.copy(last_bf16[:, a:b], planes[PACK - 1][:, a:b])
-        nc.vector.tensor_copy(grouped[0][:, :, PACK - 1], planes[PACK - 1][:].indirect(halves[0]))
-        nc.scalar.activation(grouped[1][:, :, PACK - 1], last_bf16[:].indirect(halves[1]), COPY)
+        nc.vector.tensor_copy(grouped[:, :HALF, PACK - 1], planes[PACK - 1].indirect(halves[0]))
+        nc.scalar.activation(grouped[:, HALF:, PACK - 1], last_bf16.indirect(halves[1]), COPY)
 
         for h in range(2):
-            accs = []
-            for j in range(HALF // PIECE):
-                u = h * (HALF // PIECE) + j
-                codes = keep.tile([P, PIECE], U32, name=f"codes{u}", align_bytes=64)
-                scales = keep.tile([P, PIECE], U8, name=f"scales{u}", align_bytes=64)
-                src = grouped[h][:].rearrange("p n t -> p (n t)")[:, j * PIECE * PACK : (j + 1) * PIECE * PACK]
-                nc.vector.quantize_mx(out=codes[:].bitcast(FP8X4), scales=scales[:], in_=src)
-                acc = sums.tile([P, PIECE], F32, name=f"acc{u}")
+            flat = grouped[:, h * HALF : (h + 1) * HALF, :].rearrange("p n t -> p (n t)")
+            pieces = []
+            a = 0
+            for j, n in enumerate(PIECES[h]):
+                codes = keep.tile([P, n], U32, name=f"codes{h}{j}", align_bytes=64)
+                scales = keep.tile([P, n], U8, name=f"scales{h}{j}", align_bytes=64)
+                nc.vector.quantize_mx(out=codes[:].bitcast(FP8X4), scales=scales[:], in_=flat[:, a * PACK : (a + n) * PACK])
+                acc = sums.tile([P, n], F32, name=f"acc{h}{j}")
                 nc.tensor.matmul_mx(out=acc[:], lhsT=w_codes[:].bitcast(FP8X4), lhsT_scale=w_scales[:],
                                     rhs=codes[:].bitcast(FP8X4), rhs_scale=scales[:], start=True, stop=True)
-                accs.append(acc)
-            for j, acc in enumerate(accs):
-                u = h * (HALF // PIECE) + j
-                cols = slice(u * PIECE, (u + 1) * PIECE)
-                scaled = keep.tile([P, PIECE], F32, name=f"scaled{u}")
-                nc.vector.scalar_tensor_tensor(scaled[:], acc[:], c_col[:], ts_picked[:, cols], MULT, MULT)
-                result = keep.tile([P, PIECE], F32, name=f"result{u}")
-                nc.scalar.activation(result[:], scaled[:], RELU)
-                nc.sync.dma_start(out[:, cols], result[:])
+                pieces.append((a, n, acc))
+                a += n
+            for j, (a, n, acc) in enumerate(pieces):
+                scaled = keep.tile([P, n], F32, name=f"scaled{h}{j}")
+                nc.vector.scalar_tensor_tensor(scaled[:], acc[:], c_col[:], ts_picked[h][:, a : a + n], MULT, MULT)
+                result = keep.tile([P, n], F32, name=f"result{h}{j}")
+                if n == 128:
+                    nc.vector.tensor_scalar_max(result[:], scaled[:], 0.0)
+                else:
+                    nc.scalar.activation(result[:], scaled[:], RELU)
+                nc.sync.dma_start(out[:, h * HALF + a : h * HALF + a + n], result[:])

@@ -21,10 +21,14 @@ RELU = mybir.ActivationFunctionType.Relu
 P = 128
 PACK = 4
 HALF = S // 2
-PIECES = ((256, 256), (256, 128, 128))
+PIECES = (128, 128, 256, 256, 128, 128)
+VECTOR_RELU_FROM = 768
+STEP = 128
+STORE_ENDS = (128, 384, 640, 1024)
 RUN = T // P
-LAST_CHUNKS = ((0, 1024), (1024, 2048), (2048, 3072), (3072, 3584), (3584, 3840), (3840, 4096))
-VECTOR_CHUNKS = (2, 3)
+LAST_CHUNKS = ((0, 1024), (1024, 2048), (2048, 3328), (3328, 3840), (3840, 4096))
+VECTOR_CASTS = (0, 0, 768, 256, 0)
+EARLY_CASTS = 2560
 
 
 def tile_picked_tokscale_relu_l_kernel(tc, xT, tscale, cscale, w1_words, w1_scales, offs, out):
@@ -35,12 +39,19 @@ def tile_picked_tokscale_relu_l_kernel(tc, xT, tscale, cscale, w1_words, w1_scal
         sums = ctx.enter_context(tc.psum_pool(name="sums", bufs=1))
 
         offsets = keep.tile([P, S // 16], U16, name="offsets")
-        shared = keep.tile([P, 2 * T + HALF], F32, name="shared", align_bytes=64)
-        ts_window = shared[:, 0:T]
-        grouped = shared[:, 0 : S * PACK // 2].bitcast(BF16).rearrange("p (n t) -> p n t", t=PACK)
-        pair = shared[:, T - HALF : T + HALF].rearrange("p (t n) -> p t n", t=2)
-        last_bf16 = shared[:, T - HALF : T - HALF + T // 2].bitcast(BF16)
-        planes = [keep.tile([P, T], F32, name=f"plane{t}")[:] if t != 2 else shared[:, T + HALF :] for t in range(PACK)]
+        staging = keep.tile([P, S + 2 * T], F32, name="staging", align_bytes=64)
+        ts_window = staging[:, S : S + T]
+        rows = staging[:, 0 : 2 * T].rearrange("p (t n) -> p t n", t=2)
+        dense = [rows[:, :, h * HALF : (h + 1) * HALF] for h in range(2)]
+        plane1_on = keep.tile([P, T + S], F32, name="plane1_on", align_bytes=64)
+        words = plane1_on[:, T - S :]
+        flat = words.bitcast(BF16)
+        grouped = flat.rearrange("p (n t) -> p n t", t=PACK)
+        plane0 = keep.tile([P, T], F32, name="plane0")
+        plane3 = keep.tile([P, T], F32, name="plane3")
+        planes = [plane0[:], plane1_on[:, 0:T], staging[:, S + T :], plane3[:]]
+        last_start = S + T - EARLY_CASTS // 2
+        last_bf16 = staging[:, last_start : last_start + T // 2].bitcast(BF16)
         x_rows = xT.rearrange("(p t) w -> p t w", t=PACK)
 
         ts_runs = keep.tile([P, RUN], F32, name="ts_runs")
@@ -51,15 +62,15 @@ def tile_picked_tokscale_relu_l_kernel(tc, xT, tscale, cscale, w1_words, w1_scal
         nc.vector.memset(w_scales[:].bitcast(U32), 0)
 
         nc.sync.dma_start(ts_runs[:], tscale[0].rearrange("(p c) -> p c", c=RUN))
-        nc.sync.dma_start(planes[1], x_rows[:, 1, :])
-        nc.sync.dma_start(offsets[:], offs)
         nc.sync.dma_start(planes[0], x_rows[:, 0, :])
-        for q in range(4):
-            nc.sync.dma_start(w_scales[32 * q : 32 * q + 4, :].bitcast(I32), w1_scales[0, 4 * q : 4 * q + 4, :].bitcast(I32))
+        nc.sync.dma_start(offsets[:], offs)
+        nc.sync.dma_start(planes[1], x_rows[:, 1, :])
         nc.sync.dma_start(planes[2], x_rows[:, 2, :])
         for a, b in LAST_CHUNKS:
             nc.sync.dma_start(planes[PACK - 1][:, a:b], x_rows[:, PACK - 1, a:b])
         nc.sync.dma_start(w_codes[:].bitcast(I32), w1_words[0].rearrange("p n t -> p (n t)").bitcast(I32))
+        for q in range(4):
+            nc.sync.dma_start(w_scales[32 * q : 32 * q + 4, :].bitcast(I32), w1_scales[0, 4 * q : 4 * q + 4, :].bitcast(I32))
         nc.sync.dma_start(c_col[:], cscale)
 
         identity = keep.tile([P, P], F32, name="identity")
@@ -74,44 +85,48 @@ def tile_picked_tokscale_relu_l_kernel(tc, xT, tscale, cscale, w1_words, w1_scal
             nc.scalar.activation(ts_view[:, :, 4 * b : 4 * b + 4], bank[:].rearrange("m i p -> m p i"), COPY)
 
         halves = [offsets[:, h * (HALF // 16) : (h + 1) * (HALF // 16)] for h in range(2)]
-        ts_picked = [keep.tile([P, HALF], F32, name=f"ts_picked{h}") for h in range(2)]
+        ts_picked = keep.tile([P, S], F32, name="ts_picked")
 
-        nc.vector.tensor_copy(pair[:, 1, :], planes[1].indirect(halves[1]))
-        for h in range(2):
-            nc.vector.tensor_copy(ts_picked[h][:], ts_window.indirect(halves[h]))
-        nc.vector.tensor_copy(grouped[:, :HALF, 1], planes[1].indirect(halves[0]))
-        nc.vector.tensor_copy(pair[:, 0, :], planes[0].indirect(halves[1]))
-        nc.vector.tensor_copy(grouped[:, :HALF, 0], planes[0].indirect(halves[0]))
-        nc.scalar.copy(grouped[:, HALF:, 0:2], pair.rearrange("p t n -> p n t"))
+        nc.vector.tensor_copy(rows[:, 0, 0:S], planes[0].indirect(offsets[:]))
+        nc.vector.tensor_copy(ts_picked[:], ts_window.indirect(offsets[:]))
+        for h in (1, 0):
+            nc.vector.tensor_copy(dense[h][:, 1, :], planes[1].indirect(halves[h]))
+        nc.vector.tensor_copy(grouped[:, :HALF, 0:2], dense[0].rearrange("p t n -> p n t"))
+        nc.scalar.copy(grouped[:, HALF:, 0:2], dense[1].rearrange("p t n -> p n t"))
         nc.vector.tensor_copy(grouped[:, :, 2], planes[2].indirect(offsets[:]))
 
-        for i, (a, b) in enumerate(LAST_CHUNKS):
-            if i in VECTOR_CHUNKS:
-                nc.vector.tensor_copy(last_bf16[:, a:b], planes[PACK - 1][:, a:b])
-            else:
-                nc.scalar.copy(last_bf16[:, a:b], planes[PACK - 1][:, a:b])
+        for (a, b), n in zip(LAST_CHUNKS, VECTOR_CASTS):
+            nc.scalar.copy(last_bf16[:, a : b - n], planes[PACK - 1][:, a : b - n])
+            if n:
+                nc.vector.tensor_copy(last_bf16[:, b - n : b], planes[PACK - 1][:, b - n : b])
         nc.vector.tensor_copy(grouped[:, :HALF, PACK - 1], planes[PACK - 1].indirect(halves[0]))
         nc.scalar.activation(grouped[:, HALF:, PACK - 1], last_bf16.indirect(halves[1]), COPY)
 
-        for h in range(2):
-            flat = grouped[:, h * HALF : (h + 1) * HALF, :].rearrange("p n t -> p (n t)")
-            pieces = []
-            a = 0
-            for j, n in enumerate(PIECES[h]):
-                codes = keep.tile([P, n], U32, name=f"codes{h}{j}", align_bytes=64)
-                scales = keep.tile([P, n], U8, name=f"scales{h}{j}", align_bytes=64)
-                nc.vector.quantize_mx(out=codes[:].bitcast(FP8X4), scales=scales[:], in_=flat[:, a * PACK : (a + n) * PACK])
-                acc = sums.tile([P, n], F32, name=f"acc{h}{j}")
-                nc.tensor.matmul_mx(out=acc[:], lhsT=w_codes[:].bitcast(FP8X4), lhsT_scale=w_scales[:],
-                                    rhs=codes[:].bitcast(FP8X4), rhs_scale=scales[:], start=True, stop=True)
-                pieces.append((a, n, acc))
-                a += n
-            for j, (a, n, acc) in enumerate(pieces):
-                scaled = keep.tile([P, n], F32, name=f"scaled{h}{j}")
-                nc.vector.scalar_tensor_tensor(scaled[:], acc[:], c_col[:], ts_picked[h][:, a : a + n], MULT, MULT)
-                result = keep.tile([P, n], F32, name=f"result{h}{j}")
-                if n == 128:
-                    nc.vector.tensor_scalar_max(result[:], scaled[:], 0.0)
+        pieces = []
+        a = 0
+        for j, n in enumerate(PIECES):
+            codes = keep.tile([P, n], U32, name=f"codes{j}", align_bytes=64)
+            scales = keep.tile([P, n], U8, name=f"scales{j}", align_bytes=64)
+            nc.vector.quantize_mx(out=codes[:].bitcast(FP8X4), scales=scales[:], in_=flat[:, a * PACK : (a + n) * PACK])
+            acc = spread.tile([P, n], F32, name="bank") if j < 3 else sums.tile([P, n], F32, name=f"acc{j}")
+            nc.tensor.matmul_mx(out=acc[:], lhsT=w_codes[:].bitcast(FP8X4), lhsT_scale=w_scales[:],
+                                rhs=codes[:].bitcast(FP8X4), rhs_scale=scales[:], start=True, stop=True)
+            pieces.append((a, n, acc))
+            a += n
+        scaled_late = keep.tile([P, HALF], F32, name="scaled_late")
+        scaled_halves = [words[:, S : S + HALF], scaled_late[:]]
+        results = keep.tile([P, S], F32, name="results")
+        stored = 0
+        for a, n, acc in pieces:
+            for d in range(0, n, STEP):
+                h, b = divmod(a + d, HALF)
+                done = a + d + STEP
+                scaled = scaled_halves[h][:, b : b + STEP]
+                nc.vector.scalar_tensor_tensor(scaled, acc[:, d : d + STEP], c_col[:], ts_picked[:, done - STEP : done], MULT, MULT)
+                if done > VECTOR_RELU_FROM:
+                    nc.vector.tensor_scalar_max(results[:, done - STEP : done], scaled, 0.0)
                 else:
-                    nc.scalar.activation(result[:], scaled[:], RELU)
-                nc.sync.dma_start(out[:, h * HALF + a : h * HALF + a + n], result[:])
+                    nc.scalar.activation(results[:, done - STEP : done], scaled, RELU)
+                if done in STORE_ENDS:
+                    nc.sync.dma_start(out[:, stored:done], results[:, stored:done])
+                    stored = done

@@ -21,10 +21,10 @@ RELU = mybir.ActivationFunctionType.Relu
 P = 128
 PACK = 4
 HALF = S // 2
-PIECES = (128, 128, 256, 256, 128, 128)
+PIECES = (128,) * 8
 VECTOR_RELU_FROM = 768
 STEP = 128
-STORE_ENDS = (128, 384, 640, 1024)
+STORE_ENDS = (128, 384, 640, 896, 1024)
 RUN = T // P
 LAST_CHUNKS = ((0, 1024), (1024, 2048), (2048, 3328), (3328, 3840), (3840, 4096))
 VECTOR_CASTS = (0, 0, 768, 256, 0)

@@ -26,8 +26,8 @@ VECTOR_RELU_FROM = 768
 STEP = 128
 STORE_ENDS = (128, 384, 640, 896, 1024)
 RUN = T // P
-LAST_CHUNKS = ((0, 1024), (1024, 2048), (2048, 3328), (3328, 3840), (3840, 4096))
-VECTOR_CASTS = (0, 0, 768, 256, 0)
+LAST_CHUNKS = ((0, 2816), (2816, 3840), (3840, 4096))
+VECTOR_CASTS = (1760, 704, 0)
 EARLY_CASTS = 2560
 
 

@@ -27,7 +27,7 @@ STEP = 128
 STORE_ENDS = (128, 384, 640, 896, 1024)
 RUN = T // P
 LAST_CHUNKS = ((0, 2816), (2816, 3840), (3840, 4096))
-VECTOR_CASTS = (1760, 704, 0)
+VECTOR_CASTS = (1760, 672, 0)
 EARLY_CASTS = 2560
 
 
@@ -93,7 +93,10 @@ def tile_picked_tokscale_relu_l_kernel(tc, xT, tscale, cscale, w1_words, w1_scal
             nc.vector.tensor_copy(dense[h][:, 1, :], planes[1].indirect(halves[h]))
         nc.vector.tensor_copy(grouped[:, :HALF, 0:2], dense[0].rearrange("p t n -> p n t"))
         nc.scalar.copy(grouped[:, HALF:, 0:2], dense[1].rearrange("p t n -> p n t"))
-        nc.vector.tensor_copy(grouped[:, :, 2], planes[2].indirect(offsets[:]))
+        dense2 = keep.tile([P, HALF], F32, name="dense2")
+        nc.vector.tensor_copy(dense2[:], planes[2].indirect(halves[1]))
+        nc.vector.tensor_copy(grouped[:, :HALF, 2], planes[2].indirect(halves[0]))
+        nc.scalar.copy(grouped[:, HALF:, 2], dense2[:])
 
         for (a, b), n in zip(LAST_CHUNKS, VECTOR_CASTS):
             nc.scalar.copy(last_bf16[:, a : b - n], planes[PACK - 1][:, a : b - n])

@@ -15,6 +15,7 @@ U16 = mybir.dt.uint16
 U8 = mybir.dt.uint8
 FP8X4 = mybir.dt.float8_e4m3fn_x4
 MULT = mybir.AluOpType.mult
+ADD = mybir.AluOpType.add
 COPY = mybir.ActivationFunctionType.Copy
 RELU = mybir.ActivationFunctionType.Relu
 
@@ -29,6 +30,7 @@ RUN = T // P
 LAST_CHUNKS = ((0, 2816), (2816, 3840), (3840, 4096))
 VECTOR_CASTS = (1760, 672, 0)
 EARLY_CASTS = 2560
+LAST_GATHERS = ((0, 128), (128, 320), (320, 512))
 
 
 def tile_picked_tokscale_relu_l_kernel(tc, xT, tscale, cscale, w1_words, w1_scales, offs, out):
@@ -102,7 +104,14 @@ def tile_picked_tokscale_relu_l_kernel(tc, xT, tscale, cscale, w1_words, w1_scal
             nc.scalar.copy(last_bf16[:, a : b - n], planes[PACK - 1][:, a : b - n])
             if n:
                 nc.vector.tensor_copy(last_bf16[:, b - n : b], planes[PACK - 1][:, b - n : b])
-        nc.vector.tensor_copy(grouped[:, :HALF, PACK - 1], planes[PACK - 1].indirect(halves[0]))
+        dense3 = keep.tile([P, HALF], BF16, name="dense3")
+        for a, b in LAST_GATHERS:
+            nc.vector.tensor_copy(dense3[:, a:b], planes[PACK - 1].indirect(offsets[:, a // 16 : b // 16]))
+        for i, (a, b) in enumerate(LAST_GATHERS):
+            if i == 0:
+                nc.gpsimd.tensor_scalar(grouped[:, a:b, PACK - 1], dense3[:, a:b], 1.0, 0.0, MULT, ADD)
+            else:
+                nc.vector.tensor_copy(grouped[:, a:b, PACK - 1], dense3[:, a:b])
         nc.scalar.activation(grouped[:, HALF:, PACK - 1], last_bf16.indirect(halves[1]), COPY)
 
         pieces = []

@@ -22,15 +22,13 @@ RELU = mybir.ActivationFunctionType.Relu
 P = 128
 PACK = 4
 HALF = S // 2
-PIECES = (128,) * 8
+PIECE = 128
 VECTOR_RELU_FROM = 768
-STEP = 128
 STORE_ENDS = (128, 384, 640, 896, 1024)
 RUN = T // P
-LAST_CHUNKS = ((0, 2816), (2816, 3840), (3840, 4096))
-VECTOR_CASTS = (1760, 672, 0)
-EARLY_CASTS = 2560
-LAST_GATHERS = ((0, 128), (128, 320), (320, 512))
+VECTOR_ENTRIES = (256, 768)
+GPSIMD_PIECES = ((0, 128), (128, 256))
+SCALAR_PIECES = ((768, 1024),)
 
 
 def tile_picked_tokscale_relu_l_kernel(tc, xT, tscale, cscale, w1_words, w1_scales, offs, out):
@@ -41,19 +39,16 @@ def tile_picked_tokscale_relu_l_kernel(tc, xT, tscale, cscale, w1_words, w1_scal
         sums = ctx.enter_context(tc.psum_pool(name="sums", bufs=1))
 
         offsets = keep.tile([P, S // 16], U16, name="offsets")
-        staging = keep.tile([P, S + 2 * T], F32, name="staging", align_bytes=64)
-        ts_window = staging[:, S : S + T]
-        rows = staging[:, 0 : 2 * T].rearrange("p (t n) -> p t n", t=2)
-        dense = [rows[:, :, h * HALF : (h + 1) * HALF] for h in range(2)]
-        plane1_on = keep.tile([P, T + S], F32, name="plane1_on", align_bytes=64)
-        words = plane1_on[:, T - S :]
-        flat = words.bitcast(BF16)
+        staging = keep.tile([P, 2 * T], F32, name="staging", align_bytes=64)
+        ts_window = staging[:, 0:T]
+        words = keep.tile([P, 2 * S], F32, name="words", align_bytes=64)
+        flat = words[:].bitcast(BF16)
         grouped = flat.rearrange("p (n t) -> p n t", t=PACK)
         plane0 = keep.tile([P, T], F32, name="plane0")
+        plane1 = keep.tile([P, T], F32, name="plane1")
         plane3 = keep.tile([P, T], F32, name="plane3")
-        planes = [plane0[:], plane1_on[:, 0:T], staging[:, S + T :], plane3[:]]
-        last_start = S + T - EARLY_CASTS // 2
-        last_bf16 = staging[:, last_start : last_start + T // 2].bitcast(BF16)
+        planes = [plane0[:], plane1[:], staging[:, T:], plane3[:]]
+        last = planes[PACK - 1]
         x_rows = xT.rearrange("(p t) w -> p t w", t=PACK)
 
         ts_runs = keep.tile([P, RUN], F32, name="ts_runs")
@@ -66,10 +61,8 @@ def tile_picked_tokscale_relu_l_kernel(tc, xT, tscale, cscale, w1_words, w1_scal
         nc.sync.dma_start(ts_runs[:], tscale[0].rearrange("(p c) -> p c", c=RUN))
         nc.sync.dma_start(planes[0], x_rows[:, 0, :])
         nc.sync.dma_start(offsets[:], offs)
-        nc.sync.dma_start(planes[1], x_rows[:, 1, :])
-        nc.sync.dma_start(planes[2], x_rows[:, 2, :])
-        for a, b in LAST_CHUNKS:
-            nc.sync.dma_start(planes[PACK - 1][:, a:b], x_rows[:, PACK - 1, a:b])
+        for t in range(1, PACK):
+            nc.sync.dma_start(planes[t], x_rows[:, t, :])
         nc.sync.dma_start(w_codes[:].bitcast(I32), w1_words[0].rearrange("p n t -> p (n t)").bitcast(I32))
         for q in range(4):
             nc.sync.dma_start(w_scales[32 * q : 32 * q + 4, :].bitcast(I32), w1_scales[0, 4 * q : 4 * q + 4, :].bitcast(I32))
@@ -86,59 +79,50 @@ def tile_picked_tokscale_relu_l_kernel(tc, xT, tscale, cscale, w1_words, w1_scal
                 nc.tensor.transpose(bank[:, i, :], ts_runs[:, c : c + 1].to_broadcast([P, P]), identity[:])
             nc.scalar.activation(ts_view[:, :, 4 * b : 4 * b + 4], bank[:].rearrange("m i p -> m p i"), COPY)
 
-        halves = [offsets[:, h * (HALF // 16) : (h + 1) * (HALF // 16)] for h in range(2)]
+        def entries(a, b):
+            return offsets[:, a // 16 : b // 16]
+
         ts_picked = keep.tile([P, S], F32, name="ts_picked")
+        nc.scalar.activation(ts_picked[:], ts_window.indirect(offsets[:]), COPY)
 
-        nc.vector.tensor_copy(rows[:, 0, 0:S], planes[0].indirect(offsets[:]))
-        nc.vector.tensor_copy(ts_picked[:], ts_window.indirect(offsets[:]))
-        for h in (1, 0):
-            nc.vector.tensor_copy(dense[h][:, 1, :], planes[1].indirect(halves[h]))
-        nc.vector.tensor_copy(grouped[:, :HALF, 0:2], dense[0].rearrange("p t n -> p n t"))
-        nc.scalar.copy(grouped[:, HALF:, 0:2], dense[1].rearrange("p t n -> p n t"))
-        dense2 = keep.tile([P, HALF], F32, name="dense2")
-        nc.vector.tensor_copy(dense2[:], planes[2].indirect(halves[1]))
-        nc.vector.tensor_copy(grouped[:, :HALF, 2], planes[2].indirect(halves[0]))
-        nc.scalar.copy(grouped[:, HALF:, 2], dense2[:])
+        for t in range(PACK - 1):
+            nc.vector.tensor_copy(grouped[:, :, t], planes[t].indirect(offsets[:]))
 
-        for (a, b), n in zip(LAST_CHUNKS, VECTOR_CASTS):
-            nc.scalar.copy(last_bf16[:, a : b - n], planes[PACK - 1][:, a : b - n])
-            if n:
-                nc.vector.tensor_copy(last_bf16[:, b - n : b], planes[PACK - 1][:, b - n : b])
-        dense3 = keep.tile([P, HALF], BF16, name="dense3")
-        for a, b in LAST_GATHERS:
-            nc.vector.tensor_copy(dense3[:, a:b], planes[PACK - 1].indirect(offsets[:, a // 16 : b // 16]))
-        for i, (a, b) in enumerate(LAST_GATHERS):
-            if i == 0:
-                nc.gpsimd.tensor_scalar(grouped[:, a:b, PACK - 1], dense3[:, a:b], 1.0, 0.0, MULT, ADD)
+        a, b = VECTOR_ENTRIES
+        nc.vector.tensor_copy(grouped[:, a:b, PACK - 1], last.indirect(entries(a, b)))
+        end = 2 * T + 64
+        for a, b in GPSIMD_PIECES + SCALAR_PIECES:
+            dense = staging[:].bitcast(BF16)[:, end - (b - a) : end]
+            end -= b - a
+            nc.scalar.activation(dense, last.indirect(entries(a, b)), COPY)
+            if (a, b) in GPSIMD_PIECES:
+                nc.gpsimd.tensor_scalar(grouped[:, a:b, PACK - 1], dense, 1.0, 0.0, MULT, ADD)
             else:
-                nc.vector.tensor_copy(grouped[:, a:b, PACK - 1], dense3[:, a:b])
-        nc.scalar.activation(grouped[:, HALF:, PACK - 1], last_bf16.indirect(halves[1]), COPY)
+                nc.scalar.copy(grouped[:, a:b, PACK - 1], dense)
 
-        pieces = []
-        a = 0
-        for j, n in enumerate(PIECES):
-            codes = keep.tile([P, n], U32, name=f"codes{j}", align_bytes=64)
-            scales = keep.tile([P, n], U8, name=f"scales{j}", align_bytes=64)
-            nc.vector.quantize_mx(out=codes[:].bitcast(FP8X4), scales=scales[:], in_=flat[:, a * PACK : (a + n) * PACK])
-            acc = spread.tile([P, n], F32, name="bank") if j < 3 else sums.tile([P, n], F32, name=f"acc{j}")
+        accs = []
+        for j in range(S // PIECE):
+            a = j * PIECE
+            codes = keep.tile([P, PIECE], U32, name=f"codes{j}", align_bytes=64)
+            scales = keep.tile([P, PIECE], U8, name=f"scales{j}", align_bytes=64)
+            nc.vector.quantize_mx(out=codes[:].bitcast(FP8X4), scales=scales[:], in_=flat[:, a * PACK : (a + PIECE) * PACK])
+            acc = spread.tile([P, PIECE], F32, name="bank") if j < 3 else sums.tile([P, PIECE], F32, name=f"acc{j}")
             nc.tensor.matmul_mx(out=acc[:], lhsT=w_codes[:].bitcast(FP8X4), lhsT_scale=w_scales[:],
                                 rhs=codes[:].bitcast(FP8X4), rhs_scale=scales[:], start=True, stop=True)
-            pieces.append((a, n, acc))
-            a += n
+            accs.append(acc)
         scaled_late = keep.tile([P, HALF], F32, name="scaled_late")
-        scaled_halves = [words[:, S : S + HALF], scaled_late[:]]
+        scaled_halves = [words[:, S + HALF :], scaled_late[:]]
         results = keep.tile([P, S], F32, name="results")
         stored = 0
-        for a, n, acc in pieces:
-            for d in range(0, n, STEP):
-                h, b = divmod(a + d, HALF)
-                done = a + d + STEP
-                scaled = scaled_halves[h][:, b : b + STEP]
-                nc.vector.scalar_tensor_tensor(scaled, acc[:, d : d + STEP], c_col[:], ts_picked[:, done - STEP : done], MULT, MULT)
-                if done > VECTOR_RELU_FROM:
-                    nc.vector.tensor_scalar_max(results[:, done - STEP : done], scaled, 0.0)
-                else:
-                    nc.scalar.activation(results[:, done - STEP : done], scaled, RELU)
-                if done in STORE_ENDS:
-                    nc.sync.dma_start(out[:, stored:done], results[:, stored:done])
-                    stored = done
+        for j, acc in enumerate(accs):
+            a, done = j * PIECE, (j + 1) * PIECE
+            h, b = divmod(a, HALF)
+            scaled = scaled_halves[h][:, b : b + PIECE]
+            nc.vector.scalar_tensor_tensor(scaled, acc[:], c_col[:], ts_picked[:, a:done], MULT, MULT)
+            if done > VECTOR_RELU_FROM:
+                nc.vector.tensor_scalar_max(results[:, a:done], scaled, 0.0)
+            else:
+                nc.scalar.activation(results[:, a:done], scaled, RELU)
+            if done in STORE_ENDS:
+                nc.sync.dma_start(out[:, stored:done], results[:, stored:done])
+                stored = done

@@ -26,9 +26,10 @@ PIECE = 128
 VECTOR_RELU_FROM = 768
 STORE_ENDS = (128, 384, 640, 896, 1024)
 RUN = T // P
-VECTOR_ENTRIES = (256, 768)
-GPSIMD_PIECES = ((0, 128), (128, 256))
-SCALAR_PIECES = ((768, 1024),)
+GPSIMD_ENTRIES = (0, 160)
+VECTOR_ENTRIES = (160, 672)
+SCALAR_PIECES = ((672, 896), (896, 1024))
+QUANTISER_ENDS = (128, 384, 640, 896, 1024)
 
 
 def tile_picked_tokscale_relu_l_kernel(tc, xT, tscale, cscale, w1_words, w1_scales, offs, out):
@@ -41,13 +42,13 @@ def tile_picked_tokscale_relu_l_kernel(tc, xT, tscale, cscale, w1_words, w1_scal
         offsets = keep.tile([P, S // 16], U16, name="offsets")
         staging = keep.tile([P, 2 * T], F32, name="staging", align_bytes=64)
         ts_window = staging[:, 0:T]
-        words = keep.tile([P, 2 * S], F32, name="words", align_bytes=64)
-        flat = words[:].bitcast(BF16)
+        words = staging[:, 0 : 2 * S]
+        picked = staging[:, 2 * S : T]
+        flat = words.bitcast(BF16)
         grouped = flat.rearrange("p (n t) -> p n t", t=PACK)
-        plane0 = keep.tile([P, T], F32, name="plane0")
-        plane1 = keep.tile([P, T], F32, name="plane1")
+        pair = keep.tile([P, 2 * T], F32, name="pair")
         plane3 = keep.tile([P, T], F32, name="plane3")
-        planes = [plane0[:], plane1[:], staging[:, T:], plane3[:]]
+        planes = [pair[:, 0:T], pair[:, T:], staging[:, T:], plane3[:]]
         last = planes[PACK - 1]
         x_rows = xT.rearrange("(p t) w -> p t w", t=PACK)
 
@@ -59,9 +60,9 @@ def tile_picked_tokscale_relu_l_kernel(tc, xT, tscale, cscale, w1_words, w1_scal
         nc.vector.memset(w_scales[:].bitcast(U32), 0)
 
         nc.sync.dma_start(ts_runs[:], tscale[0].rearrange("(p c) -> p c", c=RUN))
-        nc.sync.dma_start(planes[0], x_rows[:, 0, :])
         nc.sync.dma_start(offsets[:], offs)
-        for t in range(1, PACK):
+        nc.sync.dma_start(pair[:], xT.rearrange("(p t) w -> p (t w)", t=PACK)[:, 0 : 2 * T])
+        for t in range(2, PACK):
             nc.sync.dma_start(planes[t], x_rows[:, t, :])
         nc.sync.dma_start(w_codes[:].bitcast(I32), w1_words[0].rearrange("p n t -> p (n t)").bitcast(I32))
         for q in range(4):
@@ -85,33 +86,40 @@ def tile_picked_tokscale_relu_l_kernel(tc, xT, tscale, cscale, w1_words, w1_scal
         ts_picked = keep.tile([P, S], F32, name="ts_picked")
         nc.scalar.activation(ts_picked[:], ts_window.indirect(offsets[:]), COPY)
 
-        for t in range(PACK - 1):
-            nc.vector.tensor_copy(grouped[:, :, t], planes[t].indirect(offsets[:]))
+        nc.vector.tensor_copy(picked[:, 0:S], planes[0].indirect(offsets[:]))
+        nc.scalar.activation(picked[:, S:], planes[1].indirect(offsets[:]), COPY)
+        nc.scalar.copy(grouped[:, :, 0:2], picked.rearrange("p (t n) -> p n t", t=2))
+        nc.vector.tensor_copy(grouped[:, :, 2], planes[2].indirect(offsets[:]))
 
         a, b = VECTOR_ENTRIES
         nc.vector.tensor_copy(grouped[:, a:b, PACK - 1], last.indirect(entries(a, b)))
         end = 2 * T + 64
-        for a, b in GPSIMD_PIECES + SCALAR_PIECES:
-            dense = staging[:].bitcast(BF16)[:, end - (b - a) : end]
+        dense = {}
+        for a, b in (GPSIMD_ENTRIES,) + SCALAR_PIECES:
+            dense[a] = staging[:].bitcast(BF16)[:, end - (b - a) : end]
             end -= b - a
-            nc.scalar.activation(dense, last.indirect(entries(a, b)), COPY)
-            if (a, b) in GPSIMD_PIECES:
-                nc.gpsimd.tensor_scalar(grouped[:, a:b, PACK - 1], dense, 1.0, 0.0, MULT, ADD)
-            else:
-                nc.scalar.copy(grouped[:, a:b, PACK - 1], dense)
+            nc.scalar.activation(dense[a], last.indirect(entries(a, b)), COPY)
+        a, b = GPSIMD_ENTRIES
+        nc.gpsimd.tensor_scalar(grouped[:, a:b, PACK - 1], dense[a], 1.0, 0.0, MULT, ADD)
+        for a, b in SCALAR_PIECES:
+            nc.scalar.copy(grouped[:, a:b, PACK - 1], dense[a])
 
         accs = []
-        for j in range(S // PIECE):
-            a = j * PIECE
-            codes = keep.tile([P, PIECE], U32, name=f"codes{j}", align_bytes=64)
-            scales = keep.tile([P, PIECE], U8, name=f"scales{j}", align_bytes=64)
-            nc.vector.quantize_mx(out=codes[:].bitcast(FP8X4), scales=scales[:], in_=flat[:, a * PACK : (a + PIECE) * PACK])
-            acc = spread.tile([P, PIECE], F32, name="bank") if j < 3 else sums.tile([P, PIECE], F32, name=f"acc{j}")
-            nc.tensor.matmul_mx(out=acc[:], lhsT=w_codes[:].bitcast(FP8X4), lhsT_scale=w_scales[:],
-                                rhs=codes[:].bitcast(FP8X4), rhs_scale=scales[:], start=True, stop=True)
-            accs.append(acc)
+        a = 0
+        for b in QUANTISER_ENDS:
+            codes = keep.tile([P, b - a], U32, name=f"codes{a}", align_bytes=64)
+            scales = keep.tile([P, b - a], U8, name=f"scales{a}", align_bytes=64)
+            nc.vector.quantize_mx(out=codes[:].bitcast(FP8X4), scales=scales[:], in_=flat[:, a * PACK : b * PACK])
+            for d in range(0, b - a, PIECE):
+                j = len(accs)
+                acc = spread.tile([P, PIECE], F32, name="bank") if j < 3 else sums.tile([P, PIECE], F32, name=f"acc{j}")
+                nc.tensor.matmul_mx(out=acc[:], lhsT=w_codes[:].bitcast(FP8X4), lhsT_scale=w_scales[:],
+                                    rhs=codes[:, d : d + PIECE].bitcast(FP8X4), rhs_scale=scales[:, d : d + PIECE],
+                                    start=True, stop=True)
+                accs.append(acc)
+            a = b
         scaled_late = keep.tile([P, HALF], F32, name="scaled_late")
-        scaled_halves = [words[:, S + HALF :], scaled_late[:]]
+        scaled_halves = [words[:, 2 * QUANTISER_ENDS[1] : 2 * QUANTISER_ENDS[2]], scaled_late[:]]
         results = keep.tile([P, S], F32, name="results")
         stored = 0
         for j, acc in enumerate(accs):

@@ -59,9 +59,9 @@ def tile_picked_tokscale_relu_l_kernel(tc, xT, tscale, cscale, w1_words, w1_scal
 
         nc.vector.memset(w_scales[:].bitcast(U32), 0)
 
-        nc.sync.dma_start(ts_runs[:], tscale[0].rearrange("(p c) -> p c", c=RUN))
-        nc.sync.dma_start(offsets[:], offs)
+        nc.scalar.dma_start(ts_runs[:], tscale[0].rearrange("(p c) -> p c", c=RUN))
         nc.sync.dma_start(pair[:], xT.rearrange("(p t) w -> p (t w)", t=PACK)[:, 0 : 2 * T])
+        nc.sync.dma_start(offsets[:], offs)
         for t in range(2, PACK):
             nc.sync.dma_start(planes[t], x_rows[:, t, :])
         nc.sync.dma_start(w_codes[:].bitcast(I32), w1_words[0].rearrange("p n t -> p (n t)").bitcast(I32))
@@ -84,7 +84,8 @@ def tile_picked_tokscale_relu_l_kernel(tc, xT, tscale, cscale, w1_words, w1_scal
             return offsets[:, a // 16 : b // 16]
 
         ts_picked = keep.tile([P, S], F32, name="ts_picked")
-        nc.scalar.activation(ts_picked[:], ts_window.indirect(offsets[:]), COPY)
+        nc.vector.tensor_copy(ts_picked[:, 0:HALF], ts_window.indirect(entries(0, HALF)))
+        nc.scalar.activation(ts_picked[:, HALF:], ts_window.indirect(entries(HALF, S)), COPY)
 
         nc.vector.tensor_copy(picked[:, 0:S], planes[0].indirect(offsets[:]))
         nc.scalar.activation(picked[:, S:], planes[1].indirect(offsets[:]), COPY)

@@ -26,10 +26,10 @@ PIECE = 128
 VECTOR_RELU_FROM = 768
 STORE_ENDS = (128, 384, 640, 896, 1024)
 RUN = T // P
-GPSIMD_ENTRIES = (0, 160)
-VECTOR_ENTRIES = (160, 672)
-SCALAR_PIECES = ((672, 896), (896, 1024))
-QUANTISER_ENDS = (128, 384, 640, 896, 1024)
+GPSIMD_ENTRIES = 160
+VECTOR_ENTRIES = (256, 768)
+SCALAR_PIECES = ((0, 256), (768, 1024))
+QUANTISER_ENDS = (128, 256, 512, 768, 1024)
 
 
 def tile_picked_tokscale_relu_l_kernel(tc, xT, tscale, cscale, w1_words, w1_scales, offs, out):
@@ -96,14 +96,14 @@ def tile_picked_tokscale_relu_l_kernel(tc, xT, tscale, cscale, w1_words, w1_scal
         nc.vector.tensor_copy(grouped[:, a:b, PACK - 1], last.indirect(entries(a, b)))
         end = 2 * T + 64
         dense = {}
-        for a, b in (GPSIMD_ENTRIES,) + SCALAR_PIECES:
+        for a, b in SCALAR_PIECES:
             dense[a] = staging[:].bitcast(BF16)[:, end - (b - a) : end]
             end -= b - a
             nc.scalar.activation(dense[a], last.indirect(entries(a, b)), COPY)
-        a, b = GPSIMD_ENTRIES
-        nc.gpsimd.tensor_scalar(grouped[:, a:b, PACK - 1], dense[a], 1.0, 0.0, MULT, ADD)
-        for a, b in SCALAR_PIECES:
-            nc.scalar.copy(grouped[:, a:b, PACK - 1], dense[a])
+        (first, first_end), (second, second_end) = SCALAR_PIECES
+        nc.gpsimd.tensor_scalar(grouped[:, 0:GPSIMD_ENTRIES, PACK - 1], dense[0][:, 0:GPSIMD_ENTRIES], 1.0, 0.0, MULT, ADD)
+        nc.scalar.copy(grouped[:, GPSIMD_ENTRIES:first_end, PACK - 1], dense[0][:, GPSIMD_ENTRIES:])
+        nc.scalar.copy(grouped[:, second:second_end, PACK - 1], dense[second])
 
         accs = []
         a = 0
@@ -120,7 +120,7 @@ def tile_picked_tokscale_relu_l_kernel(tc, xT, tscale, cscale, w1_words, w1_scal
                 accs.append(acc)
             a = b
         scaled_late = keep.tile([P, HALF], F32, name="scaled_late")
-        scaled_halves = [words[:, 2 * QUANTISER_ENDS[1] : 2 * QUANTISER_ENDS[2]], scaled_late[:]]
+        scaled_halves = [words[:, 2 * QUANTISER_ENDS[2] : 2 * QUANTISER_ENDS[3]], scaled_late[:]]
         results = keep.tile([P, S], F32, name="results")
         stored = 0
         for j, acc in enumerate(accs):

@@ -23,7 +23,7 @@ P = 128
 PACK = 4
 HALF = S // 2
 PIECE = 128
-VECTOR_RELU_FROM = 768
+VECTOR_RELU_FROM = 896
 STORE_ENDS = (128, 384, 640, 896, 1024)
 RUN = T // P
 GPSIMD_ENTRIES = 160

@@ -24,7 +24,7 @@ PACK = 4
 HALF = S // 2
 PIECE = 128
 VECTOR_RELU_FROM = 896
-STORE_ENDS = (128, 384, 640, 896, 1024)
+STORE_ENDS = (128, 384, 640, 1024)
 RUN = T // P
 GPSIMD_ENTRIES = 160
 VECTOR_ENTRIES = (256, 768)

@@ -29,7 +29,7 @@ RUN = T // P
 GPSIMD_ENTRIES = 160
 VECTOR_ENTRIES = (256, 768)
 SCALAR_PIECES = ((0, 256), (768, 1024))
-QUANTISER_ENDS = (128, 256, 512, 768, 1024)
+QUANTISER_ENDS = (128, 256, 512, 768, 896, 1024)
 
 
 def tile_picked_tokscale_relu_l_kernel(tc, xT, tscale, cscale, w1_words, w1_scales, offs, out):
@@ -103,11 +103,12 @@ def tile_picked_tokscale_relu_l_kernel(tc, xT, tscale, cscale, w1_words, w1_scal
         (first, first_end), (second, second_end) = SCALAR_PIECES
         nc.gpsimd.tensor_scalar(grouped[:, 0:GPSIMD_ENTRIES, PACK - 1], dense[0][:, 0:GPSIMD_ENTRIES], 1.0, 0.0, MULT, ADD)
         nc.scalar.copy(grouped[:, GPSIMD_ENTRIES:first_end, PACK - 1], dense[0][:, GPSIMD_ENTRIES:])
-        nc.scalar.copy(grouped[:, second:second_end, PACK - 1], dense[second])
+        for d in range(0, second_end - second, PIECE):
+            nc.scalar.copy(grouped[:, second + d : second + d + PIECE, PACK - 1], dense[second][:, d : d + PIECE])
 
         accs = []
-        a = 0
-        for b in QUANTISER_ENDS:
+
+        def quantise_and_multiply(a, b):
             codes = keep.tile([P, b - a], U32, name=f"codes{a}", align_bytes=64)
             scales = keep.tile([P, b - a], U8, name=f"scales{a}", align_bytes=64)
             nc.vector.quantize_mx(out=codes[:].bitcast(FP8X4), scales=scales[:], in_=flat[:, a * PACK : b * PACK])
@@ -118,20 +119,28 @@ def tile_picked_tokscale_relu_l_kernel(tc, xT, tscale, cscale, w1_words, w1_scal
                                     rhs=codes[:, d : d + PIECE].bitcast(FP8X4), rhs_scale=scales[:, d : d + PIECE],
                                     start=True, stop=True)
                 accs.append(acc)
-            a = b
+
         scaled_late = keep.tile([P, HALF], F32, name="scaled_late")
-        scaled_halves = [words[:, 2 * QUANTISER_ENDS[2] : 2 * QUANTISER_ENDS[3]], scaled_late[:]]
+        homes = [words[:, 512:640], words[:, 1024:1152], words[:, 1152:1280], words[:, 1280:1408]]
+        homes.extend(scaled_late[:, d : d + PIECE] for d in range(0, HALF, PIECE))
         results = keep.tile([P, S], F32, name="results")
-        stored = 0
-        for j, acc in enumerate(accs):
+
+        def read(j):
             a, done = j * PIECE, (j + 1) * PIECE
-            h, b = divmod(a, HALF)
-            scaled = scaled_halves[h][:, b : b + PIECE]
-            nc.vector.scalar_tensor_tensor(scaled, acc[:], c_col[:], ts_picked[:, a:done], MULT, MULT)
+            nc.vector.scalar_tensor_tensor(homes[j], accs[j][:], c_col[:], ts_picked[:, a:done], MULT, MULT)
             if done > VECTOR_RELU_FROM:
-                nc.vector.tensor_scalar_max(results[:, a:done], scaled, 0.0)
+                nc.vector.tensor_scalar_max(results[:, a:done], homes[j], 0.0)
             else:
-                nc.scalar.activation(results[:, a:done], scaled, RELU)
+                nc.scalar.activation(results[:, a:done], homes[j], RELU)
             if done in STORE_ENDS:
+                stored = max(e for e in (0,) + STORE_ENDS if e < done)
                 nc.sync.dma_start(out[:, stored:done], results[:, stored:done])
-                stored = done
+
+        a = 0
+        for b in QUANTISER_ENDS[:-1]:
+            quantise_and_multiply(a, b)
+            a = b
+        read(0)
+        quantise_and_multiply(a, S)
+        for j in range(1, S // PIECE):
+            read(j)

@@ -27,6 +27,7 @@ VECTOR_RELU_FROM = 896
 STORE_ENDS = (128, 384, 640, 1024)
 RUN = T // P
 GPSIMD_ENTRIES = 160
+VECTOR_SCALES = 768
 VECTOR_ENTRIES = (256, 768)
 SCALAR_PIECES = ((0, 256), (768, 1024))
 QUANTISER_ENDS = (128, 256, 512, 768, 896, 1024)
@@ -40,26 +41,26 @@ def tile_picked_tokscale_relu_l_kernel(tc, xT, tscale, cscale, w1_words, w1_scal
         sums = ctx.enter_context(tc.psum_pool(name="sums", bufs=1))
 
         offsets = keep.tile([P, S // 16], U16, name="offsets")
-        staging = keep.tile([P, 2 * T], F32, name="staging", align_bytes=64)
+        staging = keep.tile([P, 2 * T + 2 * S], F32, name="staging", align_bytes=64)
         ts_window = staging[:, 0:T]
         words = staging[:, 0 : 2 * S]
-        picked = staging[:, 2 * S : T]
+        picked = staging[:, T : T + 2 * S]
         flat = words.bitcast(BF16)
         grouped = flat.rearrange("p (n t) -> p n t", t=PACK)
         pair = keep.tile([P, 2 * T], F32, name="pair")
         plane3 = keep.tile([P, T], F32, name="plane3")
-        planes = [pair[:, 0:T], pair[:, T:], staging[:, T:], plane3[:]]
+        planes = [pair[:, 0:T], pair[:, T:], staging[:, T + 2 * S :], plane3[:]]
         last = planes[PACK - 1]
         x_rows = xT.rearrange("(p t) w -> p t w", t=PACK)
 
-        ts_runs = keep.tile([P, RUN], F32, name="ts_runs")
+        ts_runs = picked[:, S : S + RUN]
         w_codes = keep.tile([P, N], U32, name="w_codes", align_bytes=64)
         w_scales = keep.tile([P, N], U8, name="w_scales", align_bytes=64)
         c_col = keep.tile([P, 1], F32, name="c_col")
 
         nc.vector.memset(w_scales[:].bitcast(U32), 0)
 
-        nc.scalar.dma_start(ts_runs[:], tscale[0].rearrange("(p c) -> p c", c=RUN))
+        nc.scalar.dma_start(ts_runs, tscale[0].rearrange("(p c) -> p c", c=RUN))
         nc.sync.dma_start(pair[:], xT.rearrange("(p t) w -> p (t w)", t=PACK)[:, 0 : 2 * T])
         nc.sync.dma_start(offsets[:], offs)
         for t in range(2, PACK):
@@ -84,17 +85,16 @@ def tile_picked_tokscale_relu_l_kernel(tc, xT, tscale, cscale, w1_words, w1_scal
             return offsets[:, a // 16 : b // 16]
 
         ts_picked = keep.tile([P, S], F32, name="ts_picked")
-        nc.vector.tensor_copy(ts_picked[:, 0:HALF], ts_window.indirect(entries(0, HALF)))
-        nc.scalar.activation(ts_picked[:, HALF:], ts_window.indirect(entries(HALF, S)), COPY)
-
         nc.vector.tensor_copy(picked[:, 0:S], planes[0].indirect(offsets[:]))
+        nc.vector.tensor_copy(ts_picked[:, 0:VECTOR_SCALES], ts_window.indirect(entries(0, VECTOR_SCALES)))
+        nc.scalar.activation(ts_picked[:, VECTOR_SCALES:], ts_window.indirect(entries(VECTOR_SCALES, S)), COPY)
         nc.scalar.activation(picked[:, S:], planes[1].indirect(offsets[:]), COPY)
         nc.scalar.copy(grouped[:, :, 0:2], picked.rearrange("p (t n) -> p n t", t=2))
         nc.vector.tensor_copy(grouped[:, :, 2], planes[2].indirect(offsets[:]))
 
         a, b = VECTOR_ENTRIES
         nc.vector.tensor_copy(grouped[:, a:b, PACK - 1], last.indirect(entries(a, b)))
-        end = 2 * T + 64
+        end = 2 * (T + 2 * S) + 64
         dense = {}
         for a, b in SCALAR_PIECES:
             dense[a] = staging[:].bitcast(BF16)[:, end - (b - a) : end]

@@ -15,7 +15,6 @@ U16 = mybir.dt.uint16
 U8 = mybir.dt.uint8
 FP8X4 = mybir.dt.float8_e4m3fn_x4
 MULT = mybir.AluOpType.mult
-ADD = mybir.AluOpType.add
 COPY = mybir.ActivationFunctionType.Copy
 RELU = mybir.ActivationFunctionType.Relu
 
@@ -26,10 +25,7 @@ PIECE = 128
 VECTOR_RELU_FROM = 896
 STORE_ENDS = (128, 384, 640, 1024)
 RUN = T // P
-GPSIMD_ENTRIES = 160
 VECTOR_SCALES = 768
-VECTOR_ENTRIES = (256, 768)
-SCALAR_PIECES = ((0, 256), (768, 1024))
 QUANTISER_ENDS = (128, 256, 512, 768, 896, 1024)
 
 
@@ -37,6 +33,7 @@ def tile_picked_tokscale_relu_l_kernel(tc, xT, tscale, cscale, w1_words, w1_scal
     nc = tc.nc
     with ExitStack() as ctx:
         keep = ctx.enter_context(tc.tile_pool(name="keep", bufs=1))
+        reused = ctx.enter_context(tc.tile_pool(name="reused", bufs=1))
         spread = ctx.enter_context(tc.psum_pool(name="spread", bufs=3))
         sums = ctx.enter_context(tc.psum_pool(name="sums", bufs=1))
 
@@ -48,7 +45,7 @@ def tile_picked_tokscale_relu_l_kernel(tc, xT, tscale, cscale, w1_words, w1_scal
         flat = words.bitcast(BF16)
         grouped = flat.rearrange("p (n t) -> p n t", t=PACK)
         pair = keep.tile([P, 2 * T], F32, name="pair")
-        plane3 = keep.tile([P, T], F32, name="plane3")
+        plane3 = reused.tile([P, T], F32, name="plane3", offset=0, align_bytes=64)
         planes = [pair[:, 0:T], pair[:, T:], staging[:, T + 2 * S :], plane3[:]]
         last = planes[PACK - 1]
         x_rows = xT.rearrange("(p t) w -> p t w", t=PACK)
@@ -92,24 +89,19 @@ def tile_picked_tokscale_relu_l_kernel(tc, xT, tscale, cscale, w1_words, w1_scal
         nc.scalar.copy(grouped[:, :, 0:2], picked.rearrange("p (t n) -> p n t", t=2))
         nc.vector.tensor_copy(grouped[:, :, 2], planes[2].indirect(offsets[:]))
 
-        a, b = VECTOR_ENTRIES
-        nc.vector.tensor_copy(grouped[:, a:b, PACK - 1], last.indirect(entries(a, b)))
+        nc.vector.tensor_copy(grouped[:, 0:HALF, PACK - 1], last.indirect(entries(0, HALF)))
         end = 2 * (T + 2 * S) + 64
-        dense = {}
-        for a, b in SCALAR_PIECES:
-            dense[a] = staging[:].bitcast(BF16)[:, end - (b - a) : end]
-            end -= b - a
-            nc.scalar.activation(dense[a], last.indirect(entries(a, b)), COPY)
-        (first, first_end), (second, second_end) = SCALAR_PIECES
-        nc.gpsimd.tensor_scalar(grouped[:, 0:GPSIMD_ENTRIES, PACK - 1], dense[0][:, 0:GPSIMD_ENTRIES], 1.0, 0.0, MULT, ADD)
-        nc.scalar.copy(grouped[:, GPSIMD_ENTRIES:first_end, PACK - 1], dense[0][:, GPSIMD_ENTRIES:])
-        for d in range(0, second_end - second, PIECE):
-            nc.scalar.copy(grouped[:, second + d : second + d + PIECE, PACK - 1], dense[second][:, d : d + PIECE])
+        dense = staging[:].bitcast(BF16)[:, end - HALF : end]
+        for d in range(0, HALF, HALF // 2):
+            nc.scalar.activation(dense[:, d : d + HALF // 2], last.indirect(entries(HALF + d, HALF + d + HALF // 2)), COPY)
+        nc.vector.tensor_copy(grouped[:, HALF : HALF + PIECE, PACK - 1], dense[:, 0:PIECE])
+        for d in range(PIECE, HALF, PIECE):
+            nc.scalar.copy(grouped[:, HALF + d : HALF + d + PIECE, PACK - 1], dense[:, d : d + PIECE])
 
         accs = []
 
         def quantise_and_multiply(a, b):
-            codes = keep.tile([P, b - a], U32, name=f"codes{a}", align_bytes=64)
+            codes = reused.tile([P, b - a], U32, name=f"codes{a}", offset=4 * a, align_bytes=64)
             scales = keep.tile([P, b - a], U8, name=f"scales{a}", align_bytes=64)
             nc.vector.quantize_mx(out=codes[:].bitcast(FP8X4), scales=scales[:], in_=flat[:, a * PACK : b * PACK])
             for d in range(0, b - a, PIECE):

@@ -15,18 +15,18 @@ U16 = mybir.dt.uint16
 U8 = mybir.dt.uint8
 FP8X4 = mybir.dt.float8_e4m3fn_x4
 MULT = mybir.AluOpType.mult
+ADD = mybir.AluOpType.add
 COPY = mybir.ActivationFunctionType.Copy
 RELU = mybir.ActivationFunctionType.Relu
 
 P = 128
 PACK = 4
-HALF = S // 2
 PIECE = 128
-VECTOR_RELU_FROM = 896
-STORE_ENDS = (128, 384, 640, 1024)
 RUN = T // P
 VECTOR_SCALES = 768
-QUANTISER_ENDS = (128, 256, 512, 768, 896, 1024)
+PLANE_BYTES = 4 * T
+LAST_DONE = 512
+STORE_FROM = {128: 0, 768: 512, 1024: 768, 512: 128}
 
 
 def tile_picked_tokscale_relu_l_kernel(tc, xT, tscale, cscale, w1_words, w1_scales, offs, out):
@@ -38,7 +38,7 @@ def tile_picked_tokscale_relu_l_kernel(tc, xT, tscale, cscale, w1_words, w1_scal
         sums = ctx.enter_context(tc.psum_pool(name="sums", bufs=1))
 
         offsets = keep.tile([P, S // 16], U16, name="offsets")
-        staging = keep.tile([P, 2 * T + 2 * S], F32, name="staging", align_bytes=64)
+        staging = keep.tile([P, T + 2 * S], F32, name="staging", align_bytes=64)
         ts_window = staging[:, 0:T]
         words = staging[:, 0 : 2 * S]
         picked = staging[:, T : T + 2 * S]
@@ -46,7 +46,8 @@ def tile_picked_tokscale_relu_l_kernel(tc, xT, tscale, cscale, w1_words, w1_scal
         grouped = flat.rearrange("p (n t) -> p n t", t=PACK)
         pair = keep.tile([P, 2 * T], F32, name="pair")
         plane3 = reused.tile([P, T], F32, name="plane3", offset=0, align_bytes=64)
-        planes = [pair[:, 0:T], pair[:, T:], staging[:, T + 2 * S :], plane3[:]]
+        plane2 = reused.tile([P, T], F32, name="plane2", offset=PLANE_BYTES, align_bytes=64)
+        planes = [pair[:, 0:T], pair[:, T:], plane2[:], plane3[:]]
         last = planes[PACK - 1]
         x_rows = xT.rearrange("(p t) w -> p t w", t=PACK)
 
@@ -89,50 +90,58 @@ def tile_picked_tokscale_relu_l_kernel(tc, xT, tscale, cscale, w1_words, w1_scal
         nc.scalar.copy(grouped[:, :, 0:2], picked.rearrange("p (t n) -> p n t", t=2))
         nc.vector.tensor_copy(grouped[:, :, 2], planes[2].indirect(offsets[:]))
 
-        nc.vector.tensor_copy(grouped[:, 0:HALF, PACK - 1], last.indirect(entries(0, HALF)))
-        end = 2 * (T + 2 * S) + 64
-        dense = staging[:].bitcast(BF16)[:, end - HALF : end]
-        for d in range(0, HALF, HALF // 2):
-            nc.scalar.activation(dense[:, d : d + HALF // 2], last.indirect(entries(HALF + d, HALF + d + HALF // 2)), COPY)
-        nc.vector.tensor_copy(grouped[:, HALF : HALF + PIECE, PACK - 1], dense[:, 0:PIECE])
-        for d in range(PIECE, HALF, PIECE):
-            nc.scalar.copy(grouped[:, HALF + d : HALF + d + PIECE, PACK - 1], dense[:, d : d + PIECE])
-
-        accs = []
-
-        def quantise_and_multiply(a, b):
-            codes = reused.tile([P, b - a], U32, name=f"codes{a}", offset=4 * a, align_bytes=64)
-            scales = keep.tile([P, b - a], U8, name=f"scales{a}", align_bytes=64)
-            nc.vector.quantize_mx(out=codes[:].bitcast(FP8X4), scales=scales[:], in_=flat[:, a * PACK : b * PACK])
-            for d in range(0, b - a, PIECE):
-                j = len(accs)
-                acc = spread.tile([P, PIECE], F32, name="bank") if j < 3 else sums.tile([P, PIECE], F32, name=f"acc{j}")
-                nc.tensor.matmul_mx(out=acc[:], lhsT=w_codes[:].bitcast(FP8X4), lhsT_scale=w_scales[:],
-                                    rhs=codes[:, d : d + PIECE].bitcast(FP8X4), rhs_scale=scales[:, d : d + PIECE],
-                                    start=True, stop=True)
-                accs.append(acc)
-
-        scaled_late = keep.tile([P, HALF], F32, name="scaled_late")
-        homes = [words[:, 512:640], words[:, 1024:1152], words[:, 1152:1280], words[:, 1280:1408]]
-        homes.extend(scaled_late[:, d : d + PIECE] for d in range(0, HALF, PIECE))
+        scaled = keep.tile([P, S], F32, name="scaled")
         results = keep.tile([P, S], F32, name="results")
+        sums_of = {}
 
-        def read(j):
-            a, done = j * PIECE, (j + 1) * PIECE
-            nc.vector.scalar_tensor_tensor(homes[j], accs[j][:], c_col[:], ts_picked[:, a:done], MULT, MULT)
-            if done > VECTOR_RELU_FROM:
-                nc.vector.tensor_scalar_max(results[:, a:done], homes[j], 0.0)
+        def quantise(a, b, codes, scales=None):
+            if scales is None:
+                scales = keep.tile([P, b - a], U8, name=f"scales{a}", align_bytes=64)
+            nc.vector.quantize_mx(out=codes.bitcast(FP8X4), scales=scales[:], in_=flat[:, a * PACK : b * PACK])
+            for d in range(0, b - a, PIECE):
+                width = min(PIECE, b - a - d)
+                j = len(sums_of)
+                acc = spread.tile([P, width], F32, name="bank") if j < 3 else sums.tile([P, width], F32, name=f"acc{j}")
+                nc.tensor.matmul_mx(out=acc[:], lhsT=w_codes[:].bitcast(FP8X4), lhsT_scale=w_scales[:],
+                                    rhs=codes[:, d : d + width].bitcast(FP8X4), rhs_scale=scales[:, d : d + width],
+                                    start=True, stop=True)
+                sums_of[a + d] = (acc, a + d + width)
+
+        def read(a):
+            acc, done = sums_of[a]
+            nc.vector.scalar_tensor_tensor(scaled[:, a:done], acc[:], c_col[:], ts_picked[:, a:done], MULT, MULT)
+            if done == LAST_DONE:
+                nc.vector.tensor_scalar_max(results[:, a:done], scaled[:, a:done], 0.0)
             else:
-                nc.scalar.activation(results[:, a:done], homes[j], RELU)
-            if done in STORE_ENDS:
-                stored = max(e for e in (0,) + STORE_ENDS if e < done)
+                nc.scalar.activation(results[:, a:done], scaled[:, a:done], RELU)
+            if done in STORE_FROM:
+                stored = STORE_FROM[done]
                 nc.sync.dma_start(out[:, stored:done], results[:, stored:done])
 
-        a = 0
-        for b in QUANTISER_ENDS[:-1]:
-            quantise_and_multiply(a, b)
-            a = b
-        read(0)
-        quantise_and_multiply(a, S)
-        for j in range(1, S // PIECE):
-            read(j)
+        def placed(dtype, width, at, name):
+            return reused.tile([P, width], dtype, name=name, offset=PLANE_BYTES + at, align_bytes=64)
+
+        first = placed(BF16, 192, 2048, "first")
+        second = placed(BF16, 192, 4096, "second")
+        third = placed(BF16, PIECE, 4096 + 384, "third")
+        codes_a = keep.tile([P, PIECE], U32, name="codes_a", align_bytes=64)
+        codes_bc = keep.tile([P, 2 * PIECE], U32, name="codes_bc", align_bytes=64)
+        codes_d = keep.tile([P, PIECE], U32, name="codes_d", align_bytes=64)
+        codes_v01 = placed(U32, 2 * PIECE, 2048 + 128 - 1024, "codes_v01")
+        codes_v23 = placed(U32, 2 * PIECE, 2048 + 128, "codes_v23")
+
+        nc.vector.tensor_copy(grouped[:, 512:1024, PACK - 1], last.indirect(entries(512, 1024)))
+        nc.scalar.activation(first[:], last.indirect(entries(0, 192)), COPY)
+        nc.scalar.activation(second[:], last.indirect(entries(192, 384)), COPY)
+        nc.scalar.activation(third[:], last.indirect(entries(384, 512)), COPY)
+        nc.gpsimd.tensor_scalar(grouped[:, 0:192, PACK - 1], first[:], 1.0, 0.0, MULT, ADD)
+        nc.scalar.copy(grouped[:, 192:256, PACK - 1], second[:, 0:64])
+        nc.scalar.copy(grouped[:, 256:384, PACK - 1], second[:, 64:192])
+        nc.scalar.copy(grouped[:, 384:512, PACK - 1], third[:])
+        quantise(0, 128, codes_a[:])
+        quantise(512, 768, codes_v01[:])
+        quantise(768, 1024, codes_v23[:])
+        quantise(128, 384, codes_bc[:])
+        quantise(384, 512, codes_d[:])
+        for a in (0, 512, 640, 768, 896, 128, 256, 384):
+            read(a)

@@ -121,9 +121,9 @@ def tile_picked_tokscale_relu_l_kernel(tc, xT, tscale, cscale, w1_words, w1_scal
         def placed(dtype, width, at, name):
             return reused.tile([P, width], dtype, name=name, offset=PLANE_BYTES + at, align_bytes=64)
 
-        first = placed(BF16, 192, 2048, "first")
-        second = placed(BF16, 192, 4096, "second")
-        third = placed(BF16, PIECE, 4096 + 384, "third")
+        first = placed(BF16, 160, 2048, "first")
+        second = placed(BF16, 224, 4096, "second")
+        third = placed(BF16, PIECE, 4096 + 512, "third")
         codes_a = keep.tile([P, PIECE], U32, name="codes_a", align_bytes=64)
         codes_bc = keep.tile([P, 2 * PIECE], U32, name="codes_bc", align_bytes=64)
         codes_d = keep.tile([P, PIECE], U32, name="codes_d", align_bytes=64)
@@ -131,12 +131,12 @@ def tile_picked_tokscale_relu_l_kernel(tc, xT, tscale, cscale, w1_words, w1_scal
         codes_v23 = placed(U32, 2 * PIECE, 2048 + 128, "codes_v23")
 
         nc.vector.tensor_copy(grouped[:, 512:1024, PACK - 1], last.indirect(entries(512, 1024)))
-        nc.scalar.activation(first[:], last.indirect(entries(0, 192)), COPY)
-        nc.scalar.activation(second[:], last.indirect(entries(192, 384)), COPY)
+        nc.scalar.activation(first[:], last.indirect(entries(0, 160)), COPY)
+        nc.scalar.activation(second[:], last.indirect(entries(160, 384)), COPY)
         nc.scalar.activation(third[:], last.indirect(entries(384, 512)), COPY)
-        nc.gpsimd.tensor_scalar(grouped[:, 0:192, PACK - 1], first[:], 1.0, 0.0, MULT, ADD)
-        nc.scalar.copy(grouped[:, 192:256, PACK - 1], second[:, 0:64])
-        nc.scalar.copy(grouped[:, 256:384, PACK - 1], second[:, 64:192])
+        nc.gpsimd.tensor_scalar(grouped[:, 0:160, PACK - 1], first[:], 1.0, 0.0, MULT, ADD)
+        nc.scalar.copy(grouped[:, 160:256, PACK - 1], second[:, 0:96])
+        nc.scalar.copy(grouped[:, 256:384, PACK - 1], second[:, 96:])
         nc.scalar.copy(grouped[:, 384:512, PACK - 1], third[:])
         quantise(0, 128, codes_a[:])
         quantise(512, 768, codes_v01[:])

@@ -135,7 +135,8 @@ def tile_picked_tokscale_relu_l_kernel(tc, xT, tscale, cscale, w1_words, w1_scal
         nc.scalar.activation(second[:], last.indirect(entries(160, 384)), COPY)
         nc.scalar.activation(third[:], last.indirect(entries(384, 512)), COPY)
         nc.gpsimd.tensor_scalar(grouped[:, 0:160, PACK - 1], first[:], 1.0, 0.0, MULT, ADD)
-        nc.scalar.copy(grouped[:, 160:256, PACK - 1], second[:, 0:96])
+        nc.vector.tensor_copy(grouped[:, 160:192, PACK - 1], second[:, 0:32])
+        nc.scalar.copy(grouped[:, 192:256, PACK - 1], second[:, 32:96])
         nc.scalar.copy(grouped[:, 256:384, PACK - 1], second[:, 96:])
         nc.scalar.copy(grouped[:, 384:512, PACK - 1], third[:])
         quantise(0, 128, codes_a[:])

from contextlib import ExitStack

import concourse.mybir as mybir
from concourse.masks import make_identity

K, T, S, N = 512, 4096, 1024, 128
FLOPS = 2 * K * S * N
BYTES = 4 * K * T + 4 * T + 4 * N + K * N + 16 * N + 2 * 128 * (S // 16) + 4 * N * S

F32 = mybir.dt.float32
BF16 = mybir.dt.bfloat16
I32 = mybir.dt.int32
U32 = mybir.dt.uint32
U16 = mybir.dt.uint16
U8 = mybir.dt.uint8
FP8X4 = mybir.dt.float8_e4m3fn_x4
MULT = mybir.AluOpType.mult
ADD = mybir.AluOpType.add
COPY = mybir.ActivationFunctionType.Copy
RELU = mybir.ActivationFunctionType.Relu

P = 128
PACK = 4
PIECE = 128
RUN = T // P
VECTOR_SCALES = 768
PLANE_BYTES = 4 * T
LAST_DONE = 512
STORE_FROM = {128: 0, 768: 512, 1024: 768, 512: 128}


def tile_picked_tokscale_relu_l_kernel(tc, xT, tscale, cscale, w1_words, w1_scales, offs, out):
    nc = tc.nc
    with ExitStack() as ctx:
        keep = ctx.enter_context(tc.tile_pool(name="keep", bufs=1))
        reused = ctx.enter_context(tc.tile_pool(name="reused", bufs=1))
        spread = ctx.enter_context(tc.psum_pool(name="spread", bufs=3))
        sums = ctx.enter_context(tc.psum_pool(name="sums", bufs=1))

        offsets = keep.tile([P, S // 16], U16, name="offsets")
        staging = keep.tile([P, T + 2 * S], F32, name="staging", align_bytes=64)
        ts_window = staging[:, 0:T]
        words = staging[:, 0 : 2 * S]
        picked = staging[:, T : T + 2 * S]
        flat = words.bitcast(BF16)
        grouped = flat.rearrange("p (n t) -> p n t", t=PACK)
        pair = keep.tile([P, 2 * T], F32, name="pair")
        plane3 = reused.tile([P, T], F32, name="plane3", offset=0, align_bytes=64)
        plane2 = reused.tile([P, T], F32, name="plane2", offset=PLANE_BYTES, align_bytes=64)
        planes = [pair[:, 0:T], pair[:, T:], plane2[:], plane3[:]]
        last = planes[PACK - 1]
        x_rows = xT.rearrange("(p t) w -> p t w", t=PACK)

        ts_runs = picked[:, S : S + RUN]
        w_codes = keep.tile([P, N], U32, name="w_codes", align_bytes=64)
        w_scales = keep.tile([P, N], U8, name="w_scales", align_bytes=64)
        c_col = keep.tile([P, 1], F32, name="c_col")

        nc.vector.memset(w_scales[:].bitcast(U32), 0)

        nc.scalar.dma_start(ts_runs, tscale[0].rearrange("(p c) -> p c", c=RUN))
        nc.sync.dma_start(pair[:], xT.rearrange("(p t) w -> p (t w)", t=PACK)[:, 0 : 2 * T])
        nc.sync.dma_start(offsets[:], offs)
        for t in range(2, PACK):
            nc.sync.dma_start(planes[t], x_rows[:, t, :])
        nc.sync.dma_start(w_codes[:].bitcast(I32), w1_words[0].rearrange("p n t -> p (n t)").bitcast(I32))
        for q in range(4):
            nc.sync.dma_start(w_scales[32 * q : 32 * q + 4, :].bitcast(I32), w1_scales[0, 4 * q : 4 * q + 4, :].bitcast(I32))
        nc.sync.dma_start(c_col[:], cscale)

        identity = keep.tile([P, P], F32, name="identity")
        make_identity(nc, identity[:])

        ts_view = ts_window.rearrange("m (p c) -> m p c", c=RUN)
        for b in range(RUN // 4):
            bank = spread.tile([P, 4, P], F32, name="bank")
            for i in range(4):
                c = 4 * b + i
                nc.tensor.transpose(bank[:, i, :], ts_runs[:, c : c + 1].to_broadcast([P, P]), identity[:])
            nc.scalar.activation(ts_view[:, :, 4 * b : 4 * b + 4], bank[:].rearrange("m i p -> m p i"), COPY)

        def entries(a, b):
            return offsets[:, a // 16 : b // 16]

        ts_picked = keep.tile([P, S], F32, name="ts_picked")
        nc.vector.tensor_copy(picked[:, 0:S], planes[0].indirect(offsets[:]))
        nc.vector.tensor_copy(ts_picked[:, 0:VECTOR_SCALES], ts_window.indirect(entries(0, VECTOR_SCALES)))
        nc.scalar.activation(ts_picked[:, VECTOR_SCALES:], ts_window.indirect(entries(VECTOR_SCALES, S)), COPY)
        nc.scalar.activation(picked[:, S:], planes[1].indirect(offsets[:]), COPY)
        nc.scalar.copy(grouped[:, :, 0:2], picked.rearrange("p (t n) -> p n t", t=2))
        nc.vector.tensor_copy(grouped[:, :, 2], planes[2].indirect(offsets[:]))

        scaled = keep.tile([P, S], F32, name="scaled")
        results = keep.tile([P, S], F32, name="results")
        sums_of = {}

        def quantise(a, b, codes, scales=None):
            if scales is None:
                scales = keep.tile([P, b - a], U8, name=f"scales{a}", align_bytes=64)
            nc.vector.quantize_mx(out=codes.bitcast(FP8X4), scales=scales[:], in_=flat[:, a * PACK : b * PACK])
            for d in range(0, b - a, PIECE):
                width = min(PIECE, b - a - d)
                j = len(sums_of)
                acc = spread.tile([P, width], F32, name="bank") if j < 3 else sums.tile([P, width], F32, name=f"acc{j}")
                nc.tensor.matmul_mx(out=acc[:], lhsT=w_codes[:].bitcast(FP8X4), lhsT_scale=w_scales[:],
                                    rhs=codes[:, d : d + width].bitcast(FP8X4), rhs_scale=scales[:, d : d + width],
                                    start=True, stop=True)
                sums_of[a + d] = (acc, a + d + width)

        def read(a):
            acc, done = sums_of[a]
            nc.vector.scalar_tensor_tensor(scaled[:, a:done], acc[:], c_col[:], ts_picked[:, a:done], MULT, MULT)
            if done == LAST_DONE:
                nc.vector.tensor_scalar_max(results[:, a:done], scaled[:, a:done], 0.0)
            else:
                nc.scalar.activation(results[:, a:done], scaled[:, a:done], RELU)
            if done in STORE_FROM:
                stored = STORE_FROM[done]
                nc.sync.dma_start(out[:, stored:done], results[:, stored:done])

        def placed(dtype, width, at, name):
            return reused.tile([P, width], dtype, name=name, offset=PLANE_BYTES + at, align_bytes=64)

        first = placed(BF16, 160, 2048, "first")
        second = placed(BF16, 224, 4096, "second")
        third = placed(BF16, PIECE, 4096 + 512, "third")
        codes_a = keep.tile([P, PIECE], U32, name="codes_a", align_bytes=64)
        codes_bc = keep.tile([P, 2 * PIECE], U32, name="codes_bc", align_bytes=64)
        codes_d = keep.tile([P, PIECE], U32, name="codes_d", align_bytes=64)
        codes_v01 = placed(U32, 2 * PIECE, 2048 + 128 - 1024, "codes_v01")
        codes_v23 = placed(U32, 2 * PIECE, 2048 + 128, "codes_v23")

        nc.vector.tensor_copy(grouped[:, 512:1024, PACK - 1], last.indirect(entries(512, 1024)))
        nc.scalar.activation(first[:], last.indirect(entries(0, 160)), COPY)
        nc.scalar.activation(second[:], last.indirect(entries(160, 384)), COPY)
        nc.scalar.activation(third[:], last.indirect(entries(384, 512)), COPY)
        nc.gpsimd.tensor_scalar(grouped[:, 0:160, PACK - 1], first[:], 1.0, 0.0, MULT, ADD)
        nc.vector.tensor_copy(grouped[:, 160:192, PACK - 1], second[:, 0:32])
        nc.scalar.copy(grouped[:, 192:256, PACK - 1], second[:, 32:96])
        nc.scalar.copy(grouped[:, 256:384, PACK - 1], second[:, 96:])
        nc.scalar.copy(grouped[:, 384:512, PACK - 1], third[:])
        quantise(0, 128, codes_a[:])
        quantise(512, 768, codes_v01[:])
        quantise(768, 1024, codes_v23[:])
        quantise(128, 384, codes_bc[:])
        quantise(384, 512, codes_d[:])
        for a in (0, 512, 640, 768, 896, 128, 256, 384):
            read(a)
